import numpy as np
import ml_dtypes

BF16 = ml_dtypes.bfloat16


def bf(x):
    return np.asarray(x, np.float32).astype(BF16)


def f32(x):
    return np.asarray(x, np.float32)


def f64(x):
    return np.asarray(x).astype(np.float64)


def striped(idx):
    return np.tile(idx.reshape(-1, 16).T, (8, 1))


S, K, M, N, D, V = 4096, 256, 512, 1024, 2, 512


def sigmoid(v):
    return 1.0 / (1.0 + np.exp(-v))


def setup_inputs():
    return {"table": bf(np.random.standard_normal((K, S))), "w": bf(np.random.standard_normal((D, K, M)) / np.sqrt(D * K)), "b": f32(0.5 * np.random.standard_normal((M, 1))), "offs": striped(np.random.permutation(np.tile(np.arange(S), 2))[:N])}


def reference(table, w, b, offs):
    idx = offs[:16].T.reshape(-1)
    x = f64(table)[:, idx]
    y = sum(f64(w)[t].T @ x[:, t * V : (t + 1) * V] for t in range(D))
    return (y + f64(b)) * sigmoid(y + f64(b))

@@ -1,0 +1,64 @@
+import concourse.mybir as mybir
+
+BF16, F32, U16 = mybir.dt.bfloat16, mybir.dt.float32, mybir.dt.uint16
+SILU = mybir.ActivationFunctionType.Silu
+
+P = 128
+NODES = 4096
+FEATURES = 256
+OUT_FEATURES = 512
+ENDS = 2
+EDGES = 512
+K_BLOCKS = FEATURES // P
+M_BLOCKS = OUT_FEATURES // P
+COLS_PER_END = EDGES // 16
+
+FLOPS = 2 * OUT_FEATURES * EDGES * ENDS * FEATURES
+
+
+def tile_gather_matmul_kernel(tc, table, w, b, offs, out):
+    nc = tc.nc
+    with (
+        tc.tile_pool(name="held", bufs=1) as held,
+        tc.psum_pool(name="psum", bufs=1) as psum,
+    ):
+        offsets = held.tile([P, ENDS * COLS_PER_END], U16, name="offsets")
+        nc.sync.dma_start(offsets[:], offs)
+
+        nodes = [held.tile([P, NODES], BF16, name=f"nodes{k}") for k in range(K_BLOCKS)]
+        weights = [
+            [held.tile([P, OUT_FEATURES], BF16, name=f"weights{t}_{k}") for k in range(K_BLOCKS)]
+            for t in range(ENDS)
+        ]
+        for k in range(K_BLOCKS):
+            rows = slice(k * P, (k + 1) * P)
+            nc.sync.dma_start(weights[0][k][:], w[0, rows, :])
+            nc.sync.dma_start(nodes[k][:], table[rows, :])
+            nc.sync.dma_start(weights[1][k][:], w[1, rows, :])
+
+        bias = held.tile([P, M_BLOCKS], F32, name="bias")
+        with nc.allow_non_contiguous_dma(reason="one float32 of the bias to a partition"):
+            nc.scalar.dma_start(bias[:], b.rearrange("(a p) o -> p (a o)", p=P))
+
+        def picked(k, t):
+            return nodes[k][:].indirect(offsets[:, t * COLS_PER_END : (t + 1) * COLS_PER_END])
+
+        def weight_block(t, k, a):
+            return weights[t][k][:, a * P : (a + 1) * P]
+
+        banks = [psum.tile([P, EDGES], F32, name=f"bank{a}") for a in range(M_BLOCKS)]
+
+        for t in range(ENDS):
+            for a in range(M_BLOCKS):
+                nc.tensor.matmul(
+                    banks[a][:], weight_block(t, 0, a), picked(0, t), start=(t == 0), stop=False
+                )
+
+        for a in range(M_BLOCKS):
+            for t in range(ENDS):
+                nc.tensor.matmul(
+                    banks[a][:], weight_block(t, 1, a), picked(1, t), start=False, stop=(t == ENDS - 1)
+                )
+            result = held.tile([P, EDGES], F32, name=f"result{a}")
+            nc.scalar.activation(result[:], banks[a][:], SILU, bias=bias[:, a : a + 1])
+            nc.sync.dma_start(out[a * P : (a + 1) * P, :], result[:])

@@ -13,6 +13,8 @@ K_BLOCKS = FEATURES // P
 M_BLOCKS = OUT_FEATURES // P
 COLS_PER_END = EDGES // 16
 
+WARM_UPS = 8
+
 FLOPS = 2 * OUT_FEATURES * EDGES * ENDS * FEATURES
 
 
@@ -39,6 +41,12 @@ def tile_gather_matmul_kernel(tc, table, w, b, offs, out):
         bias = held.tile([P, M_BLOCKS], F32, name="bias")
         with nc.allow_non_contiguous_dma(reason="one float32 of the bias to a partition"):
             nc.scalar.dma_start(bias[:], b.rearrange("(a p) o -> p (a o)", p=P))
+
+        zeros = held.tile([P, EDGES], BF16, name="zeros")
+        nc.vector.memset(zeros[:], 0.0)
+        unread = psum.tile([P, EDGES], F32, name="unread")
+        for i in range(WARM_UPS):
+            nc.tensor.matmul(unread[:], zeros[:, 0:P], zeros[:], start=True, stop=True)
 
         def picked(k, t):
             return nodes[k][:].indirect(offsets[:, t * COLS_PER_END : (t + 1) * COLS_PER_END])

@@ -13,8 +13,6 @@ K_BLOCKS = FEATURES // P
 M_BLOCKS = OUT_FEATURES // P
 COLS_PER_END = EDGES // 16
 
-WARM_UPS = 8
-
 FLOPS = 2 * OUT_FEATURES * EDGES * ENDS * FEATURES
 
 
@@ -40,13 +38,7 @@ def tile_gather_matmul_kernel(tc, table, w, b, offs, out):
 
         bias = held.tile([P, M_BLOCKS], F32, name="bias")
         with nc.allow_non_contiguous_dma(reason="one float32 of the bias to a partition"):
-            nc.scalar.dma_start(bias[:], b.rearrange("(a p) o -> p (a o)", p=P))
-
-        zeros = held.tile([P, EDGES], BF16, name="zeros")
-        nc.vector.memset(zeros[:], 0.0)
-        unread = psum.tile([P, EDGES], F32, name="unread")
-        for i in range(WARM_UPS):
-            nc.tensor.matmul(unread[:], zeros[:, 0:P], zeros[:], start=True, stop=True)
+            nc.sync.dma_start(bias[:], b.rearrange("(a p) o -> p (a o)", p=P))
 
         def picked(k, t):
             return nodes[k][:].indirect(offsets[:, t * COLS_PER_END : (t + 1) * COLS_PER_END])
@@ -68,5 +60,7 @@ def tile_gather_matmul_kernel(tc, table, w, b, offs, out):
                     banks[a][:], weight_block(t, 1, a), picked(1, t), start=False, stop=(t == ENDS - 1)
                 )
             result = held.tile([P, EDGES], F32, name=f"result{a}")
-            nc.scalar.activation(result[:], banks[a][:], SILU, bias=bias[:, a : a + 1])
-            nc.sync.dma_start(out[a * P : (a + 1) * P, :], result[:])
+            for half, queue in enumerate((nc.sync, nc.scalar)):
+                cols = slice(half * EDGES // 2, (half + 1) * EDGES // 2)
+                nc.scalar.activation(result[:, cols], banks[a][:, cols], SILU, bias=bias[:, a : a + 1])
+                queue.dma_start(out[a * P : (a + 1) * P, cols], result[:, cols])

@@ -26,15 +26,12 @@ def tile_gather_matmul_kernel(tc, table, w, b, offs, out):
         nc.sync.dma_start(offsets[:], offs)
 
         nodes = [held.tile([P, NODES], BF16, name=f"nodes{k}") for k in range(K_BLOCKS)]
-        weights = [
-            [held.tile([P, OUT_FEATURES], BF16, name=f"weights{t}_{k}") for k in range(K_BLOCKS)]
-            for t in range(ENDS)
-        ]
-        for k in range(K_BLOCKS):
-            rows = slice(k * P, (k + 1) * P)
-            nc.sync.dma_start(weights[0][k][:], w[0, rows, :])
-            nc.sync.dma_start(nodes[k][:], table[rows, :])
-            nc.sync.dma_start(weights[1][k][:], w[1, rows, :])
+        weights = held.tile([P, ENDS * K_BLOCKS, OUT_FEATURES], BF16, name="weights")
+        w_blocks = w.rearrange("t (k p) m -> p (t k) m", p=P)
+        nc.sync.dma_start(weights[:, :1, :], w_blocks[:, :1, :])
+        nc.sync.dma_start(nodes[0][:], table[:P, :])
+        nc.sync.dma_start(weights[:, 1:, :], w_blocks[:, 1:, :])
+        nc.sync.dma_start(nodes[1][:], table[P:, :])
 
         bias = held.tile([P, M_BLOCKS], F32, name="bias")
         with nc.allow_non_contiguous_dma(reason="one float32 of the bias to a partition"):
@@ -44,7 +41,7 @@ def tile_gather_matmul_kernel(tc, table, w, b, offs, out):
             return nodes[k][:].indirect(offsets[:, t * COLS_PER_END : (t + 1) * COLS_PER_END])
 
         def weight_block(t, k, a):
-            return weights[t][k][:, a * P : (a + 1) * P]
+            return weights[:, t * K_BLOCKS + k, a * P : (a + 1) * P]
 
         banks = [psum.tile([P, EDGES], F32, name=f"bank{a}") for a in range(M_BLOCKS)]
 

@@ -28,10 +28,12 @@ def tile_gather_matmul_kernel(tc, table, w, b, offs, out):
         nodes = [held.tile([P, NODES], BF16, name=f"nodes{k}") for k in range(K_BLOCKS)]
         weights = held.tile([P, ENDS * K_BLOCKS, OUT_FEATURES], BF16, name="weights")
         w_blocks = w.rearrange("t (k p) m -> p (t k) m", p=P)
-        nc.sync.dma_start(weights[:, :1, :], w_blocks[:, :1, :])
+        nc.sync.dma_start(weights[:, 0, :P], w_blocks[:, 0, :P])
         nc.sync.dma_start(nodes[0][:], table[:P, :])
-        nc.sync.dma_start(weights[:, 1:, :], w_blocks[:, 1:, :])
+        nc.sync.dma_start(weights[:, 0, P:], w_blocks[:, 0, P:])
+        nc.sync.dma_start(weights[:, 1:3, :], w_blocks[:, 1:3, :])
         nc.sync.dma_start(nodes[1][:], table[P:, :])
+        nc.sync.dma_start(weights[:, 3, :], w_blocks[:, 3, :])
 
         bias = held.tile([P, M_BLOCKS], F32, name="bias")
         with nc.allow_non_contiguous_dma(reason="one float32 of the bias to a partition"):

@@ -23,13 +23,13 @@ def tile_gather_matmul_kernel(tc, table, w, b, offs, out):
         tc.psum_pool(name="psum", bufs=1) as psum,
     ):
         offsets = held.tile([P, ENDS * COLS_PER_END], U16, name="offsets")
-        nc.sync.dma_start(offsets[:], offs)
-
         nodes = [held.tile([P, NODES], BF16, name=f"nodes{k}") for k in range(K_BLOCKS)]
         weights = held.tile([P, ENDS * K_BLOCKS, OUT_FEATURES], BF16, name="weights")
         w_blocks = w.rearrange("t (k p) m -> p (t k) m", p=P)
-        nc.sync.dma_start(weights[:, 0, :P], w_blocks[:, 0, :P])
+
         nc.sync.dma_start(nodes[0][:], table[:P, :])
+        nc.sync.dma_start(offsets[:], offs)
+        nc.sync.dma_start(weights[:, 0, :P], w_blocks[:, 0, :P])
         nc.sync.dma_start(weights[:, 0, P:], w_blocks[:, 0, P:])
         nc.sync.dma_start(weights[:, 1:3, :], w_blocks[:, 1:3, :])
         nc.sync.dma_start(nodes[1][:], table[P:, :])

@@ -59,7 +59,7 @@ def tile_gather_matmul_kernel(tc, table, w, b, offs, out):
                     banks[a][:], weight_block(t, 1, a), picked(1, t), start=False, stop=(t == ENDS - 1)
                 )
             result = held.tile([P, EDGES], F32, name=f"result{a}")
-            for half, queue in enumerate((nc.sync, nc.scalar)):
+            for half in range(2):
                 cols = slice(half * EDGES // 2, (half + 1) * EDGES // 2)
                 nc.scalar.activation(result[:, cols], banks[a][:, cols], SILU, bias=bias[:, a : a + 1])
-                queue.dma_start(out[a * P : (a + 1) * P, cols], result[:, cols])
+                nc.sync.dma_start(out[a * P : (a + 1) * P, cols], result[:, cols])

@@ -12,6 +12,7 @@ EDGES = 512
 K_BLOCKS = FEATURES // P
 M_BLOCKS = OUT_FEATURES // P
 COLS_PER_END = EDGES // 16
+ROW_START = 256
 
 FLOPS = 2 * OUT_FEATURES * EDGES * ENDS * FEATURES
 
@@ -23,8 +24,12 @@ def tile_gather_matmul_kernel(tc, table, w, b, offs, out):
         tc.psum_pool(name="psum", bufs=1) as psum,
     ):
         offsets = held.tile([P, ENDS * COLS_PER_END], U16, name="offsets")
-        nodes = [held.tile([P, NODES], BF16, name=f"nodes{k}") for k in range(K_BLOCKS)]
-        weights = held.tile([P, ENDS * K_BLOCKS, OUT_FEATURES], BF16, name="weights")
+        nodes = [
+            held.tile([P, NODES], BF16, name=f"nodes{k}", align_bytes=ROW_START) for k in range(K_BLOCKS)
+        ]
+        weights = held.tile(
+            [P, ENDS * K_BLOCKS, OUT_FEATURES], BF16, name="weights", align_bytes=ROW_START
+        )
         w_blocks = w.rearrange("t (k p) m -> p (t k) m", p=P)
 
         nc.sync.dma_start(nodes[0][:], table[:P, :])
@@ -58,7 +63,7 @@ def tile_gather_matmul_kernel(tc, table, w, b, offs, out):
                 nc.tensor.matmul(
                     banks[a][:], weight_block(t, 1, a), picked(1, t), start=False, stop=(t == ENDS - 1)
                 )
-            result = held.tile([P, EDGES], F32, name=f"result{a}")
+            result = held.tile([P, EDGES], F32, name=f"result{a}", align_bytes=ROW_START)
             for half in range(2):
                 cols = slice(half * EDGES // 2, (half + 1) * EDGES // 2)
                 nc.scalar.activation(result[:, cols], banks[a][:, cols], SILU, bias=bias[:, a : a + 1])

@@ -34,8 +34,8 @@ def tile_gather_matmul_kernel(tc, table, w, b, offs, out):
 
         nc.sync.dma_start(nodes[0][:], table[:P, :])
         nc.sync.dma_start(offsets[:], offs)
-        nc.sync.dma_start(weights[:, 0, :P], w_blocks[:, 0, :P])
-        nc.sync.dma_start(weights[:, 0, P:], w_blocks[:, 0, P:])
+        nc.sync.dma_start(weights[:, 0, : 2 * P], w_blocks[:, 0, : 2 * P])
+        nc.sync.dma_start(weights[:, 0, 2 * P :], w_blocks[:, 0, 2 * P :])
         nc.sync.dma_start(weights[:, 1:3, :], w_blocks[:, 1:3, :])
         nc.sync.dma_start(nodes[1][:], table[P:, :])
         nc.sync.dma_start(weights[:, 3, :], w_blocks[:, 3, :])

@@ -36,9 +36,9 @@ def tile_gather_matmul_kernel(tc, table, w, b, offs, out):
         nc.sync.dma_start(offsets[:], offs)
         nc.sync.dma_start(weights[:, 0, : 2 * P], w_blocks[:, 0, : 2 * P])
         nc.sync.dma_start(weights[:, 0, 2 * P :], w_blocks[:, 0, 2 * P :])
-        nc.sync.dma_start(weights[:, 1:3, :], w_blocks[:, 1:3, :])
+        nc.sync.dma_start(weights[:, 2, :], w_blocks[:, 2, :])
         nc.sync.dma_start(nodes[1][:], table[P:, :])
-        nc.sync.dma_start(weights[:, 3, :], w_blocks[:, 3, :])
+        nc.sync.dma_start(weights[:, 1::2, :], w_blocks[:, 1::2, :])
 
         bias = held.tile([P, M_BLOCKS], F32, name="bias")
         with nc.allow_non_contiguous_dma(reason="one float32 of the bias to a partition"):

@@ -58,11 +58,16 @@ def tile_gather_matmul_kernel(tc, table, w, b, offs, out):
                     banks[a][:], weight_block(t, 0, a), picked(0, t), start=(t == 0), stop=False
                 )
 
+        early = range(M_BLOCKS - 1)
+        last = M_BLOCKS - 1
+        for a in early:
+            nc.tensor.matmul(banks[a][:], weight_block(1, 1, a), picked(1, 1), start=False, stop=False)
+        for a in early:
+            nc.tensor.matmul(banks[a][:], weight_block(0, 1, a), picked(1, 0), start=False, stop=True)
+        nc.tensor.matmul(banks[last][:], weight_block(0, 1, last), picked(1, 0), start=False, stop=False)
+        nc.tensor.matmul(banks[last][:], weight_block(1, 1, last), picked(1, 1), start=False, stop=True)
+
         for a in range(M_BLOCKS):
-            for t in range(ENDS):
-                nc.tensor.matmul(
-                    banks[a][:], weight_block(t, 1, a), picked(1, t), start=False, stop=(t == ENDS - 1)
-                )
             result = held.tile([P, EDGES], F32, name=f"result{a}", align_bytes=ROW_START)
             for half in range(2):
                 cols = slice(half * EDGES // 2, (half + 1) * EDGES // 2)

@@ -32,17 +32,17 @@ def tile_gather_matmul_kernel(tc, table, w, b, offs, out):
         )
         w_blocks = w.rearrange("t (k p) m -> p (t k) m", p=P)
 
-        nc.sync.dma_start(nodes[0][:], table[:P, :])
         nc.sync.dma_start(offsets[:], offs)
         nc.sync.dma_start(weights[:, 0, : 2 * P], w_blocks[:, 0, : 2 * P])
-        nc.sync.dma_start(weights[:, 0, 2 * P :], w_blocks[:, 0, 2 * P :])
-        nc.sync.dma_start(weights[:, 2, :], w_blocks[:, 2, :])
-        nc.sync.dma_start(nodes[1][:], table[P:, :])
-        nc.sync.dma_start(weights[:, 1::2, :], w_blocks[:, 1::2, :])
+        nc.scalar.dma_start(nodes[0][:], table[:P, :])
 
+        nc.scalar.dma_start(weights[:, 0, 2 * P :], w_blocks[:, 0, 2 * P :])
+        nc.scalar.dma_start(weights[:, 2, :], w_blocks[:, 2, :])
+        nc.scalar.dma_start(nodes[1][:], table[P:, :])
+        nc.scalar.dma_start(weights[:, 1::2, :], w_blocks[:, 1::2, :])
         bias = held.tile([P, M_BLOCKS], F32, name="bias")
         with nc.allow_non_contiguous_dma(reason="one float32 of the bias to a partition"):
-            nc.sync.dma_start(bias[:], b.rearrange("(a p) o -> p (a o)", p=P))
+            nc.scalar.dma_start(bias[:], b.rearrange("(a p) o -> p (a o)", p=P))
 
         def picked(k, t):
             return nodes[k][:].indirect(offsets[:, t * COLS_PER_END : (t + 1) * COLS_PER_END])

import concourse.mybir as mybir

BF16, F32, U16 = mybir.dt.bfloat16, mybir.dt.float32, mybir.dt.uint16
SILU = mybir.ActivationFunctionType.Silu

P = 128
NODES = 4096
FEATURES = 256
OUT_FEATURES = 512
ENDS = 2
EDGES = 512
K_BLOCKS = FEATURES // P
M_BLOCKS = OUT_FEATURES // P
COLS_PER_END = EDGES // 16
ROW_START = 256

FLOPS = 2 * OUT_FEATURES * EDGES * ENDS * FEATURES


def tile_gather_matmul_kernel(tc, table, w, b, offs, out):
    nc = tc.nc
    with (
        tc.tile_pool(name="held", bufs=1) as held,
        tc.psum_pool(name="psum", bufs=1) as psum,
    ):
        offsets = held.tile([P, ENDS * COLS_PER_END], U16, name="offsets")
        nodes = [
            held.tile([P, NODES], BF16, name=f"nodes{k}", align_bytes=ROW_START) for k in range(K_BLOCKS)
        ]
        weights = held.tile(
            [P, ENDS * K_BLOCKS, OUT_FEATURES], BF16, name="weights", align_bytes=ROW_START
        )
        w_blocks = w.rearrange("t (k p) m -> p (t k) m", p=P)

        nc.sync.dma_start(offsets[:], offs)
        nc.sync.dma_start(weights[:, 0, : 2 * P], w_blocks[:, 0, : 2 * P])
        nc.scalar.dma_start(nodes[0][:], table[:P, :])

        nc.scalar.dma_start(weights[:, 0, 2 * P :], w_blocks[:, 0, 2 * P :])
        nc.scalar.dma_start(weights[:, 2, :], w_blocks[:, 2, :])
        nc.scalar.dma_start(nodes[1][:], table[P:, :])
        nc.scalar.dma_start(weights[:, 1::2, :], w_blocks[:, 1::2, :])
        bias = held.tile([P, M_BLOCKS], F32, name="bias")
        with nc.allow_non_contiguous_dma(reason="one float32 of the bias to a partition"):
            nc.scalar.dma_start(bias[:], b.rearrange("(a p) o -> p (a o)", p=P))

        def picked(k, t):
            return nodes[k][:].indirect(offsets[:, t * COLS_PER_END : (t + 1) * COLS_PER_END])

        def weight_block(t, k, a):
            return weights[:, t * K_BLOCKS + k, a * P : (a + 1) * P]

        banks = [psum.tile([P, EDGES], F32, name=f"bank{a}") for a in range(M_BLOCKS)]

        for t in range(ENDS):
            for a in range(M_BLOCKS):
                nc.tensor.matmul(
                    banks[a][:], weight_block(t, 0, a), picked(0, t), start=(t == 0), stop=False
                )

        early = range(M_BLOCKS - 1)
        last = M_BLOCKS - 1
        for a in early:
            nc.tensor.matmul(banks[a][:], weight_block(1, 1, a), picked(1, 1), start=False, stop=False)
        for a in early:
            nc.tensor.matmul(banks[a][:], weight_block(0, 1, a), picked(1, 0), start=False, stop=True)
        nc.tensor.matmul(banks[last][:], weight_block(0, 1, last), picked(1, 0), start=False, stop=False)
        nc.tensor.matmul(banks[last][:], weight_block(1, 1, last), picked(1, 1), start=False, stop=True)

        for a in range(M_BLOCKS):
            result = held.tile([P, EDGES], F32, name=f"result{a}", align_bytes=ROW_START)
            for half in range(2):
                cols = slice(half * EDGES // 2, (half + 1) * EDGES // 2)
                nc.scalar.activation(result[:, cols], banks[a][:, cols], SILU, bias=bias[:, a : a + 1])
                nc.sync.dma_start(out[a * P : (a + 1) * P, cols], result[:, cols])
